import numpy as np
import ml_dtypes


def mxq(x, axis, fmt="e4m3"):
    dtype, down = {"e4m3": (ml_dtypes.float8_e4m3fn, 7), "e5m2": (ml_dtypes.float8_e5m2, 14)}[fmt]
    v = np.moveaxis(np.asarray(x, np.float32).astype(ml_dtypes.bfloat16).astype(np.float64), axis, -1)
    blocks = v.reshape(v.shape[:-1] + (-1, 32))
    amax = np.abs(blocks).max(-1, keepdims=True)
    byte = np.maximum(np.where(amax > 0, np.frexp(amax)[1] - 1 + 127, 0) - down, 1)
    scale = np.exp2(byte - 127.0)
    codes = (blocks / scale).astype(np.float32).astype(dtype).astype(np.float64)
    return np.moveaxis((codes * scale).reshape(v.shape), -1, axis)


WIDE = False


def mx_kscale(k):
    if not WIDE:
        return np.ones(k)
    levels = np.array([10, -10, 5, -5, 0])
    if k % 512:
        return np.exp2(np.random.permutation(np.resize(levels, k // 32))).repeat(32)
    a = np.empty((k // 512, 16))
    for p in range(k // 512):
        a[p, :8] = np.random.permutation(np.resize(levels, 8))
        for g in range(8):
            far = levels[np.abs(levels - a[p, g]) >= 10]
            a[p, g + 8] = far[np.random.randint(len(far))]
    return np.exp2(a.ravel()).repeat(32)


def f64(x):
    return np.asarray(x).astype(np.float64)


def striped(idx):
    return np.tile(idx.reshape(-1, 16).T, (8, 1)).astype(np.uint16)


def unstriped(offs):
    return offs[:16].T.reshape(-1).astype(np.int64)


E2M1 = np.array([0.0, 0.5, 1.0, 1.5, 2.0, 3.0, 4.0, 6.0, -0.0, -0.5, -1.0, -1.5, -2.0, -3.0, -4.0, -6.0])


def pack_weight(w, fmt):
    k, n = w.shape
    w = f64(np.asarray(w, np.float32).astype(ml_dtypes.bfloat16)).reshape(k // 32, 32, n)
    amax = np.abs(w).max(1)
    if fmt == "e4m3":
        byte = np.frexp(amax)[1] - 1 + 127 - 7
    else:
        mant, ex = np.frexp(amax / 6.0)
        byte = np.where(mant > 0.5, ex, ex - 1) + 127
    byte = np.clip(np.where(amax > 0, byte, 1), 1, 254)
    scaled = (w * np.exp2(127.0 - byte)[:, None, :]).reshape(k, n).astype(np.float32)
    by_word = np.ascontiguousarray(scaled.reshape(k // 512, 128, 4, n).transpose(0, 1, 3, 2))
    if fmt == "e4m3":
        words = by_word.astype(ml_dtypes.float8_e4m3fn).view(np.uint8)
    else:
        c = by_word.astype(ml_dtypes.float4_e2m1fn).view(np.uint8) & 0xF
        words = (c[..., 0::2] | (c[..., 1::2] << 4)).reshape(k // 512, 128, 2 * n)
    return np.ascontiguousarray(words), np.ascontiguousarray(byte.astype(np.uint8).reshape(k // 512, 16, n))


def unpack_weight(words, scales, fmt):
    g, _, n = scales.shape
    words = np.ascontiguousarray(words).reshape(g, 128, n, -1)
    if fmt == "e4m3":
        vals = words.view(ml_dtypes.float8_e4m3fn).astype(np.float64)
    else:
        nib = np.empty((g, 128, n, 4), np.uint8)
        nib[..., 0::2] = words & 0xF
        nib[..., 1::2] = words >> 4
        vals = E2M1[nib]
    vals = vals * np.repeat(np.exp2(scales.astype(np.float64) - 127.0), 8, axis=1)[..., None]
    return vals.transpose(0, 1, 3, 2).reshape(g * 512, n)


K, T, E, C, N = 512, 1024, 4, 256, 512


def by_expert(wq, xq):
    return np.concatenate([wq[e].T @ xq[:, e * C:(e + 1) * C] for e in range(E)], axis=1)


def setup_inputs():
    n = np.random.standard_normal
    s = mx_kscale(K)[:, None]
    w = [pack_weight(m, "e2m1") for m in n((E, K, N)) / np.sqrt(K) / s[None]]
    return {
        "xT": (n((K, T)) * s).astype(np.float32),
        "w_words": np.stack([m[0] for m in w]),
        "w_scales": np.stack([m[1] for m in w]),
        "b": (0.3 * n((N, E))).astype(np.float32),
        "gate": np.tile(np.random.uniform(0.2, 1.0, E * C), (N, 1)).astype(np.float32),
        "offs": striped(np.random.permutation(T)[:E * C]),
        "dst": striped(np.random.permutation(T)[:E * C]),
    }


def reference(xT, w_words, w_scales, b, gate, offs, dst):
    idx = unstriped(offs)
    w = np.stack([unpack_weight(w_words[e], w_scales[e], "e2m1") for e in range(E)])
    xq = mxq(f64(xT)[:, idx], 0, "e4m3")
    y = by_expert(w, xq)
    y = y + np.repeat(f64(b), C, axis=1)
    out = np.zeros((N, T))
    out[:, unstriped(dst)] = f64(gate) * y
    return out

@@ -1,0 +1,148 @@
+from contextlib import ExitStack
+
+import concourse.mybir as mybir
+
+K, T, E, C, N = 512, 1024, 4, 256, 512
+P = 128
+PACK = 4
+N_TILES = N // P
+
+FLOPS = 2 * K * N * E * C
+BYTES = 4 * (K * T + N * E + E * C + N * T) + E * (K * N // 2 + K // 32 * N) + 2 * 2 * P * (T // 16)
+
+F32 = mybir.dt.float32
+BF16 = mybir.dt.bfloat16
+U32 = mybir.dt.uint32
+I32 = mybir.dt.int32
+U16 = mybir.dt.uint16
+U8 = mybir.dt.uint8
+FP8X4 = mybir.dt.float8_e4m3fn_x4
+FP4X4 = mybir.dt.float4_e2m1fn_x4
+COPY = mybir.ActivationFunctionType.Copy
+IDENTITY = mybir.ActivationFunctionType.Identity
+MULT = mybir.AluOpType.mult
+
+CHUNKS = ((0, 128), (128, 256), (256, 512), (512, 1024))
+
+
+def tile_moe_two_lin_bias_kernel(tc, xT, w_words, w_scales, b, gate, offs, dst, out):
+    nc = tc.nc
+    with ExitStack() as ctx:
+        held = ctx.enter_context(tc.tile_pool(name="held", bufs=1))
+        ys = ctx.enter_context(tc.tile_pool(name="ys", bufs=4))
+        psum = ctx.enter_context(tc.psum_pool(name="psum", bufs=8))
+
+        offs_t = held.tile([P, T // 16], U16, name="offs_t")
+        dst_t = held.tile([P, T // 16], U16, name="dst_t")
+        nc.sync.dma_start(offs_t[:], offs)
+
+        ws = held.tile([P, E, N], U8, name="ws", align_bytes=64)
+        nc.vector.memset(ws[:].bitcast(I32), 0)
+        scale_rows = w_scales.rearrange("e a q n -> (a q) e n").bitcast(I32)
+        for q in range(4):
+            nc.scalar.dma_start(out=ws[32 * q : 32 * q + 4].bitcast(I32), in_=scale_rows[4 * q : 4 * q + 4])
+        bias = held.tile([P, N_TILES, E], F32, name="bias")
+        nc.scalar.dma_start(out=bias[:], in_=b.rearrange("(i p) e -> p i e", p=P))
+
+        x_rows = xT.rearrange("(p j) w -> p j w", j=PACK)
+        planes = []
+        for j in range(PACK):
+            plane = held.tile([P, T], F32, name=f"plane{j}")
+            nc.sync.dma_start(out=plane[:], in_=x_rows[:, j, :])
+            planes.append(plane)
+
+        words = held.tile([P, E, 2 * N], U8, name="words", align_bytes=64)
+        word_rows = w_words.rearrange("e a p n -> p (e a) n").bitcast(I32)
+        gate_t = held.tile([P, E * C], F32, name="gate_t")
+        nc.sync.dma_start(out=words[:, 0:1].bitcast(I32), in_=word_rows[:, 0:1])
+        nc.sync.dma_start(dst_t[:], dst)
+        nc.sync.dma_start(out=gate_t[:, 0:C], in_=gate[0:P, 0:C])
+        nc.sync.dma_start(out=words[:, 1:E].bitcast(I32), in_=word_rows[:, 1:E])
+        nc.sync.dma_start(out=gate_t[:, C : E * C], in_=gate[0:P, C : E * C])
+
+        halves = [held.tile([P, T], BF16, name=f"half{j}") for j in range(PACK)]
+        grouped = [
+            held.tile([P, stop - start, PACK], BF16, name=f"grouped{c}", align_bytes=64)
+            for c, (start, stop) in enumerate(CHUNKS)
+        ]
+        codes = [held.tile([P, stop - start], U32, name=f"codes{c}", align_bytes=64) for c, (start, stop) in enumerate(CHUNKS)]
+        scales = [held.tile([P, stop - start], U8, name=f"scales{c}", align_bytes=64) for c, (start, stop) in enumerate(CHUNKS)]
+        windows = [held.tile([P, T], F32, name=f"window{i}") for i in range(N_TILES)]
+
+        def columns(listed, c):
+            start, stop = CHUNKS[c]
+            return listed[:, start // 16 : stop // 16]
+
+        def gather_vector(c, j):
+            nc.vector.tensor_copy(grouped[c][:, :, j], planes[j][:].indirect(columns(offs_t, c)))
+
+        def gather_scalar(c, j):
+            nc.scalar.activation(grouped[c][:, :, j], halves[j][:].indirect(columns(offs_t, c)), COPY)
+
+        def quantize(c):
+            nc.vector.quantize_mx(
+                out=codes[c][:].bitcast(FP8X4),
+                scales=scales[c][:],
+                in_=grouped[c][:].rearrange("p w j -> p (w j)"),
+            )
+
+        results = {}
+
+        def multiply(c, i):
+            start, stop = CHUNKS[c]
+            acc = psum.tile([P, 512], F32, name="acc")
+            y = ys.tile([P, stop - start], F32, name=f"y{c}")
+            results[c, i] = y
+            cuts = sorted({start, stop} | {e * C for e in range(E) if start < e * C < stop})
+            for lo, hi in zip(cuts, cuts[1:]):
+                e = lo // C
+                cols = slice(lo - start, hi - start)
+                nc.tensor.matmul_mx(
+                    out=acc[:, cols],
+                    lhsT=words[:, e, 2 * P * i : 2 * P * (i + 1)].bitcast(FP4X4),
+                    lhsT_scale=ws[:, e, P * i : P * (i + 1)],
+                    rhs=codes[c][:, cols].bitcast(FP8X4),
+                    rhs_scale=scales[c][:, cols],
+                    start=True,
+                    stop=True,
+                )
+            for lo, hi in zip(cuts, cuts[1:]):
+                e = lo // C
+                cols = slice(lo - start, hi - start)
+                nc.scalar.activation(y[:, cols], acc[:, cols], IDENTITY, bias=bias[:, i, e : e + 1])
+
+        def scatter(c, i):
+            start, stop = CHUNKS[c]
+            nc.vector.tensor_tensor(windows[i][:].indirect(columns(dst_t, c)), results[c, i][:], gate_t[:, start:stop], MULT)
+
+        for j in range(PACK):
+            gather_vector(0, j)
+            gather_vector(1, j)
+            if j < 3:
+                nc.scalar.activation(halves[j][:], planes[j][:], COPY)
+        quantize(0)
+        quantize(1)
+        nc.vector.tensor_copy(halves[3][:], planes[3][:])
+        gather_scalar(2, 0)
+        gather_scalar(2, 1)
+        for c in (0, 1):
+            for i in range(N_TILES):
+                multiply(c, i)
+        for c in (0, 1):
+            for i in range(N_TILES):
+                scatter(c, i)
+        gather_scalar(2, 2)
+        gather_scalar(2, 3)
+        quantize(2)
+        for i in range(N_TILES):
+            multiply(2, i)
+        for i in range(N_TILES):
+            scatter(2, i)
+        for j in range(PACK):
+            gather_scalar(3, j)
+        quantize(3)
+        for i in range(N_TILES):
+            multiply(3, i)
+        for i in range(N_TILES):
+            scatter(3, i)
+            nc.sync.dma_start(out=out[P * i : P * (i + 1), :], in_=windows[i][:])

@@ -22,127 +22,145 @@ COPY = mybir.ActivationFunctionType.Copy
 IDENTITY = mybir.ActivationFunctionType.Identity
 MULT = mybir.AluOpType.mult
 
-CHUNKS = ((0, 128), (128, 256), (256, 512), (512, 1024))
+CHUNKS = ((0, 256), (256, 512), (512, 1024))
 
 
 def tile_moe_two_lin_bias_kernel(tc, xT, w_words, w_scales, b, gate, offs, dst, out):
     nc = tc.nc
     with ExitStack() as ctx:
         held = ctx.enter_context(tc.tile_pool(name="held", bufs=1))
-        ys = ctx.enter_context(tc.tile_pool(name="ys", bufs=4))
         psum = ctx.enter_context(tc.psum_pool(name="psum", bufs=8))
 
         offs_t = held.tile([P, T // 16], U16, name="offs_t")
         dst_t = held.tile([P, T // 16], U16, name="dst_t")
-        nc.sync.dma_start(offs_t[:], offs)
-
         ws = held.tile([P, E, N], U8, name="ws", align_bytes=64)
-        nc.vector.memset(ws[:].bitcast(I32), 0)
         scale_rows = w_scales.rearrange("e a q n -> (a q) e n").bitcast(I32)
-        for q in range(4):
-            nc.scalar.dma_start(out=ws[32 * q : 32 * q + 4].bitcast(I32), in_=scale_rows[4 * q : 4 * q + 4])
         bias = held.tile([P, N_TILES, E], F32, name="bias")
-        nc.scalar.dma_start(out=bias[:], in_=b.rearrange("(i p) e -> p i e", p=P))
-
         x_rows = xT.rearrange("(p j) w -> p j w", j=PACK)
-        planes = []
-        for j in range(PACK):
-            plane = held.tile([P, T], F32, name=f"plane{j}")
-            nc.sync.dma_start(out=plane[:], in_=x_rows[:, j, :])
-            planes.append(plane)
-
+        planes = [held.tile([P, T], F32, name=f"plane{j}") for j in range(PACK)]
         words = held.tile([P, E, 2 * N], U8, name="words", align_bytes=64)
         word_rows = w_words.rearrange("e a p n -> p (e a) n").bitcast(I32)
         gate_t = held.tile([P, E * C], F32, name="gate_t")
-        nc.sync.dma_start(out=words[:, 0:1].bitcast(I32), in_=word_rows[:, 0:1])
+
+        nc.vector.memset(ws[:].bitcast(I32), 0)
+        nc.gpsimd.dma_start(out=bias[:], in_=b.rearrange("(i p) e -> p i e", p=P))
+        nc.sync.dma_start(offs_t[:], offs)
         nc.sync.dma_start(dst_t[:], dst)
+        for j in range(PACK):
+            if j == 3:
+                for q in range(4):
+                    nc.sync.dma_start(out=ws[32 * q : 32 * q + 4].bitcast(I32), in_=scale_rows[4 * q : 4 * q + 4])
+            nc.sync.dma_start(out=planes[j][:], in_=x_rows[:, j, :])
+        nc.sync.dma_start(out=words[:, 0:1].bitcast(I32), in_=word_rows[:, 0:1])
         nc.sync.dma_start(out=gate_t[:, 0:C], in_=gate[0:P, 0:C])
         nc.sync.dma_start(out=words[:, 1:E].bitcast(I32), in_=word_rows[:, 1:E])
         nc.sync.dma_start(out=gate_t[:, C : E * C], in_=gate[0:P, C : E * C])
 
-        halves = [held.tile([P, T], BF16, name=f"half{j}") for j in range(PACK)]
-        grouped = [
-            held.tile([P, stop - start, PACK], BF16, name=f"grouped{c}", align_bytes=64)
-            for c, (start, stop) in enumerate(CHUNKS)
-        ]
-        codes = [held.tile([P, stop - start], U32, name=f"codes{c}", align_bytes=64) for c, (start, stop) in enumerate(CHUNKS)]
-        scales = [held.tile([P, stop - start], U8, name=f"scales{c}", align_bytes=64) for c, (start, stop) in enumerate(CHUNKS)]
-        windows = [held.tile([P, T], F32, name=f"window{i}") for i in range(N_TILES)]
+        halves = [held.tile([P, T], BF16, name=f"half{j}") for j in range(3)]
 
-        def columns(listed, c):
-            start, stop = CHUNKS[c]
+        def columns(listed, start, stop):
             return listed[:, start // 16 : stop // 16]
 
-        def gather_vector(c, j):
-            nc.vector.tensor_copy(grouped[c][:, :, j], planes[j][:].indirect(columns(offs_t, c)))
+        def gather_vector(grouped, start, stop, j):
+            nc.vector.tensor_copy(grouped[:, :, j], planes[j][:].indirect(columns(offs_t, start, stop)))
 
-        def gather_scalar(c, j):
-            nc.scalar.activation(grouped[c][:, :, j], halves[j][:].indirect(columns(offs_t, c)), COPY)
+        def gather_scalar(grouped, start, stop, j):
+            nc.scalar.activation(grouped[:, :, j], halves[j][:].indirect(columns(offs_t, start, stop)), COPY)
 
-        def quantize(c):
+        def quantize(codes, scales, grouped, lo, hi):
             nc.vector.quantize_mx(
-                out=codes[c][:].bitcast(FP8X4),
-                scales=scales[c][:],
-                in_=grouped[c][:].rearrange("p w j -> p (w j)"),
+                out=codes[:, lo:hi].bitcast(FP8X4),
+                scales=scales[:, lo:hi],
+                in_=grouped[:, lo:hi, :].rearrange("p w j -> p (w j)"),
             )
 
-        results = {}
+        def multiply(acc, quantized, lo, hi, e, i):
+            codes, scales = quantized
+            nc.tensor.matmul_mx(
+                out=acc,
+                lhsT=words[:, e, 2 * P * i : 2 * P * (i + 1)].bitcast(FP4X4),
+                lhsT_scale=ws[:, e, P * i : P * (i + 1)],
+                rhs=codes[:, lo:hi].bitcast(FP8X4),
+                rhs_scale=scales[:, lo:hi],
+                start=True,
+                stop=True,
+            )
 
-        def multiply(c, i):
-            start, stop = CHUNKS[c]
-            acc = psum.tile([P, 512], F32, name="acc")
-            y = ys.tile([P, stop - start], F32, name=f"y{c}")
-            results[c, i] = y
-            cuts = sorted({start, stop} | {e * C for e in range(E) if start < e * C < stop})
-            for lo, hi in zip(cuts, cuts[1:]):
-                e = lo // C
-                cols = slice(lo - start, hi - start)
-                nc.tensor.matmul_mx(
-                    out=acc[:, cols],
-                    lhsT=words[:, e, 2 * P * i : 2 * P * (i + 1)].bitcast(FP4X4),
-                    lhsT_scale=ws[:, e, P * i : P * (i + 1)],
-                    rhs=codes[c][:, cols].bitcast(FP8X4),
-                    rhs_scale=scales[c][:, cols],
-                    start=True,
-                    stop=True,
+        def add_bias(y, acc, e, i):
+            nc.scalar.activation(y, acc, IDENTITY, bias=bias[:, i, e : e + 1])
+
+        def scatter(window, y, start, stop):
+            nc.vector.tensor_tensor(window[:].indirect(columns(dst_t, start, stop)), y, gate_t[:, start:stop], MULT)
+
+        grouped0 = held.tile([P, C, PACK], BF16, name="grouped0", tag="g0", align_bytes=64)
+        grouped1 = held.tile([P, C, PACK], BF16, name="grouped1", tag="w2", align_bytes=64)
+        codes = [held.tile([P, n], U32, name=f"codes{c}", align_bytes=64) for c, n in enumerate((256, 256, 512))]
+        scales = [held.tile([P, n], U8, name=f"scales{c}", align_bytes=64) for c, n in enumerate((256, 256, 512))]
+        q = list(zip(codes, scales))
+        w0 = held.tile([P, T], F32, name="w0")
+        w1 = held.tile([P, T], F32, name="w1")
+        ya = held.tile([P, 128], F32, name="ya", tag="w3", align_bytes=64)
+        yb = held.tile([P, 128], F32, name="yb")
+        y01 = held.tile([P, C], F32, name="y01")
+        y02 = held.tile([P, C], F32, name="y02")
+        y3 = held.tile([P, 2 * C], F32, name="y3")
+        y1 = [held.tile([P, C], F32, name=f"y1{i}") for i in range(3)]
+        y2 = [held.tile([P, 2 * C], F32, name=f"y2{i}") for i in range(4)]
+
+        def gather0(j):
+            for lo in (0, 128):
+                nc.vector.tensor_copy(
+                    grouped0[:, lo : lo + 128, j], planes[j][:].indirect(columns(offs_t, lo, lo + 128))
                 )
-            for lo, hi in zip(cuts, cuts[1:]):
-                e = lo // C
-                cols = slice(lo - start, hi - start)
-                nc.scalar.activation(y[:, cols], acc[:, cols], IDENTITY, bias=bias[:, i, e : e + 1])
 
-        def scatter(c, i):
-            start, stop = CHUNKS[c]
-            nc.vector.tensor_tensor(windows[i][:].indirect(columns(dst_t, c)), results[c, i][:], gate_t[:, start:stop], MULT)
-
-        for j in range(PACK):
-            gather_vector(0, j)
-            gather_vector(1, j)
-            if j < 3:
-                nc.scalar.activation(halves[j][:], planes[j][:], COPY)
-        quantize(0)
-        quantize(1)
+        for j in range(3):
+            gather0(j)
+            nc.scalar.activation(halves[j][:], planes[j][:], COPY)
+        gather0(3)
+        quantize(codes[0], scales[0], grouped0, 0, 128)
+        quantize(codes[0], scales[0], grouped0, 128, 256)
+        halves.append(held.tile([P, T], BF16, name="half3", tag="g0", align_bytes=64))
         nc.vector.tensor_copy(halves[3][:], planes[3][:])
-        gather_scalar(2, 0)
-        gather_scalar(2, 1)
-        for c in (0, 1):
-            for i in range(N_TILES):
-                multiply(c, i)
-        for c in (0, 1):
-            for i in range(N_TILES):
-                scatter(c, i)
-        gather_scalar(2, 2)
-        gather_scalar(2, 3)
-        quantize(2)
-        for i in range(N_TILES):
-            multiply(2, i)
-        for i in range(N_TILES):
-            scatter(2, i)
+        acc = psum.tile([P, 512], F32, name="acc")
+        multiply(acc[:, 0:128], q[0], 0, 128, 0, 0)
+        add_bias(ya[:], acc[:, 0:128], 0, 0)
+        for i, y in ((1, y01[:]), (2, y02[:]), (3, y3[:, 0:C])):
+            acc = psum.tile([P, 512], F32, name="acc")
+            multiply(acc[:, 0:C], q[0], 0, C, 0, i)
+            add_bias(y, acc[:, 0:C], 0, i)
+            if i == 1:
+                acc = psum.tile([P, 512], F32, name="acc")
+                multiply(acc[:, 0:128], q[0], 128, C, 0, 0)
+                add_bias(yb[:], acc[:, 0:128], 0, 0)
         for j in range(PACK):
-            gather_scalar(3, j)
-        quantize(3)
+            gather_scalar(grouped1, 256, 512, j)
+        scatter(w0, ya[:], 0, 128)
+        scatter(w1, y01[:], 0, 256)
+        scatter(w0, yb[:], 128, 256)
+        quantize(codes[1], scales[1], grouped1, 0, C)
+        for i, y in enumerate((y1[0][:], y1[1][:], y1[2][:], y3[:, C : 2 * C])):
+            acc = psum.tile([P, 512], F32, name="acc")
+            multiply(acc[:, 0:C], q[1], 0, C, 1, i)
+            add_bias(y, acc[:, 0:C], 1, i)
+        w2 = held.tile([P, T], F32, name="w2", tag="w2", align_bytes=64)
+        scatter(w2, y02[:], 0, 256)
+        grouped2 = held.tile([P, 2 * C, PACK], BF16, name="grouped2", tag="w3", align_bytes=64)
+        for j in range(PACK):
+            gather_scalar(grouped2, 512, 1024, j)
+        scatter(w0, y1[0][:], 256, 512)
+        scatter(w1, y1[1][:], 256, 512)
+        scatter(w2, y1[2][:], 256, 512)
+        quantize(codes[2], scales[2], grouped2, 0, 2 * C)
         for i in range(N_TILES):
-            multiply(3, i)
-        for i in range(N_TILES):
-            scatter(3, i)
-            nc.sync.dma_start(out=out[P * i : P * (i + 1), :], in_=windows[i][:])
+            acc = psum.tile([P, 512], F32, name="acc")
+            for e in (2, 3):
+                lo = (e - 2) * C
+                multiply(acc[:, lo : lo + C], q[2], lo, lo + C, e, i)
+            for e in (2, 3):
+                lo = (e - 2) * C
+                add_bias(y2[i][:, lo : lo + C], acc[:, lo : lo + C], e, i)
+        w3 = held.tile([P, T], F32, name="w3", tag="w3", align_bytes=64)
+        scatter(w3, y3[:], 0, 512)
+        for i, window in enumerate((w0, w1, w2, w3)):
+            scatter(window, y2[i][:], 512, 1024)
+            nc.sync.dma_start(out=out[P * i : P * (i + 1), :], in_=window[:])

@@ -21,6 +21,7 @@ FP4X4 = mybir.dt.float4_e2m1fn_x4
 COPY = mybir.ActivationFunctionType.Copy
 IDENTITY = mybir.ActivationFunctionType.Identity
 MULT = mybir.AluOpType.mult
+ADD = mybir.AluOpType.add
 
 CHUNKS = ((0, 256), (256, 512), (512, 1024))
 
@@ -43,15 +44,14 @@ def tile_moe_two_lin_bias_kernel(tc, xT, w_words, w_scales, b, gate, offs, dst, 
         gate_t = held.tile([P, E * C], F32, name="gate_t")
 
         nc.vector.memset(ws[:].bitcast(I32), 0)
-        nc.gpsimd.dma_start(out=bias[:], in_=b.rearrange("(i p) e -> p i e", p=P))
         nc.sync.dma_start(offs_t[:], offs)
         nc.sync.dma_start(dst_t[:], dst)
         for j in range(PACK):
-            if j == 3:
-                for q in range(4):
-                    nc.sync.dma_start(out=ws[32 * q : 32 * q + 4].bitcast(I32), in_=scale_rows[4 * q : 4 * q + 4])
             nc.sync.dma_start(out=planes[j][:], in_=x_rows[:, j, :])
         nc.sync.dma_start(out=words[:, 0:1].bitcast(I32), in_=word_rows[:, 0:1])
+        for q in range(4):
+            nc.sync.dma_start(out=ws[32 * q : 32 * q + 4].bitcast(I32), in_=scale_rows[4 * q : 4 * q + 4])
+        nc.sync.dma_start(out=bias[:], in_=b.rearrange("(i p) e -> p i e", p=P))
         nc.sync.dma_start(out=gate_t[:, 0:C], in_=gate[0:P, 0:C])
         nc.sync.dma_start(out=words[:, 1:E].bitcast(I32), in_=word_rows[:, 1:E])
         nc.sync.dma_start(out=gate_t[:, C : E * C], in_=gate[0:P, C : E * C])
@@ -108,14 +108,12 @@ def tile_moe_two_lin_bias_kernel(tc, xT, w_words, w_scales, b, gate, offs, dst, 
         y2 = [held.tile([P, 2 * C], F32, name=f"y2{i}") for i in range(4)]
 
         def gather0(j):
-            for lo in (0, 128):
-                nc.vector.tensor_copy(
-                    grouped0[:, lo : lo + 128, j], planes[j][:].indirect(columns(offs_t, lo, lo + 128))
-                )
+            for lo, hi in ((0, 128), (128, 256)) if j == 3 else ((0, 256),):
+                nc.vector.tensor_copy(grouped0[:, lo:hi, j], planes[j][:].indirect(columns(offs_t, lo, hi)))
 
         for j in range(3):
             gather0(j)
-            nc.scalar.activation(halves[j][:], planes[j][:], COPY)
+            nc.gpsimd.tensor_scalar(halves[j][:], planes[j][:], 1.0, 0.0, op0=MULT, op1=ADD)
         gather0(3)
         quantize(codes[0], scales[0], grouped0, 0, 128)
         quantize(codes[0], scales[0], grouped0, 128, 256)

from contextlib import ExitStack

import concourse.mybir as mybir

K, T, E, C, N = 512, 1024, 4, 256, 512
P = 128
PACK = 4
N_TILES = N // P

FLOPS = 2 * K * N * E * C
BYTES = 4 * (K * T + N * E + E * C + N * T) + E * (K * N // 2 + K // 32 * N) + 2 * 2 * P * (T // 16)

F32 = mybir.dt.float32
BF16 = mybir.dt.bfloat16
U32 = mybir.dt.uint32
I32 = mybir.dt.int32
U16 = mybir.dt.uint16
U8 = mybir.dt.uint8
FP8X4 = mybir.dt.float8_e4m3fn_x4
FP4X4 = mybir.dt.float4_e2m1fn_x4
COPY = mybir.ActivationFunctionType.Copy
IDENTITY = mybir.ActivationFunctionType.Identity
MULT = mybir.AluOpType.mult
ADD = mybir.AluOpType.add

CHUNKS = ((0, 256), (256, 512), (512, 1024))


def tile_moe_two_lin_bias_kernel(tc, xT, w_words, w_scales, b, gate, offs, dst, out):
    nc = tc.nc
    with ExitStack() as ctx:
        held = ctx.enter_context(tc.tile_pool(name="held", bufs=1))
        psum = ctx.enter_context(tc.psum_pool(name="psum", bufs=8))

        offs_t = held.tile([P, T // 16], U16, name="offs_t")
        dst_t = held.tile([P, T // 16], U16, name="dst_t")
        ws = held.tile([P, E, N], U8, name="ws", align_bytes=64)
        scale_rows = w_scales.rearrange("e a q n -> (a q) e n").bitcast(I32)
        bias = held.tile([P, N_TILES, E], F32, name="bias")
        x_rows = xT.rearrange("(p j) w -> p j w", j=PACK)
        planes = [held.tile([P, T], F32, name=f"plane{j}") for j in range(PACK)]
        words = held.tile([P, E, 2 * N], U8, name="words", align_bytes=64)
        word_rows = w_words.rearrange("e a p n -> p (e a) n").bitcast(I32)
        gate_t = held.tile([P, E * C], F32, name="gate_t")

        nc.vector.memset(ws[:].bitcast(I32), 0)
        nc.sync.dma_start(offs_t[:], offs)
        nc.sync.dma_start(dst_t[:], dst)
        for j in range(PACK):
            nc.sync.dma_start(out=planes[j][:], in_=x_rows[:, j, :])
        nc.sync.dma_start(out=words[:, 0:1].bitcast(I32), in_=word_rows[:, 0:1])
        for q in range(4):
            nc.sync.dma_start(out=ws[32 * q : 32 * q + 4].bitcast(I32), in_=scale_rows[4 * q : 4 * q + 4])
        nc.sync.dma_start(out=bias[:], in_=b.rearrange("(i p) e -> p i e", p=P))
        nc.sync.dma_start(out=gate_t[:, 0:C], in_=gate[0:P, 0:C])
        nc.sync.dma_start(out=words[:, 1:E].bitcast(I32), in_=word_rows[:, 1:E])
        nc.sync.dma_start(out=gate_t[:, C : E * C], in_=gate[0:P, C : E * C])

        halves = [held.tile([P, T], BF16, name=f"half{j}") for j in range(3)]

        def columns(listed, start, stop):
            return listed[:, start // 16 : stop // 16]

        def gather_vector(grouped, start, stop, j):
            nc.vector.tensor_copy(grouped[:, :, j], planes[j][:].indirect(columns(offs_t, start, stop)))

        def gather_scalar(grouped, start, stop, j):
            nc.scalar.activation(grouped[:, :, j], halves[j][:].indirect(columns(offs_t, start, stop)), COPY)

        def quantize(codes, scales, grouped, lo, hi):
            nc.vector.quantize_mx(
                out=codes[:, lo:hi].bitcast(FP8X4),
                scales=scales[:, lo:hi],
                in_=grouped[:, lo:hi, :].rearrange("p w j -> p (w j)"),
            )

        def multiply(acc, quantized, lo, hi, e, i):
            codes, scales = quantized
            nc.tensor.matmul_mx(
                out=acc,
                lhsT=words[:, e, 2 * P * i : 2 * P * (i + 1)].bitcast(FP4X4),
                lhsT_scale=ws[:, e, P * i : P * (i + 1)],
                rhs=codes[:, lo:hi].bitcast(FP8X4),
                rhs_scale=scales[:, lo:hi],
                start=True,
                stop=True,
            )

        def add_bias(y, acc, e, i):
            nc.scalar.activation(y, acc, IDENTITY, bias=bias[:, i, e : e + 1])

        def scatter(window, y, start, stop):
            nc.vector.tensor_tensor(window[:].indirect(columns(dst_t, start, stop)), y, gate_t[:, start:stop], MULT)

        grouped0 = held.tile([P, C, PACK], BF16, name="grouped0", tag="g0", align_bytes=64)
        grouped1 = held.tile([P, C, PACK], BF16, name="grouped1", tag="w2", align_bytes=64)
        codes = [held.tile([P, n], U32, name=f"codes{c}", align_bytes=64) for c, n in enumerate((256, 256, 512))]
        scales = [held.tile([P, n], U8, name=f"scales{c}", align_bytes=64) for c, n in enumerate((256, 256, 512))]
        q = list(zip(codes, scales))
        w0 = held.tile([P, T], F32, name="w0")
        w1 = held.tile([P, T], F32, name="w1")
        ya = held.tile([P, 128], F32, name="ya", tag="w3", align_bytes=64)
        yb = held.tile([P, 128], F32, name="yb")
        y01 = held.tile([P, C], F32, name="y01")
        y02 = held.tile([P, C], F32, name="y02")
        y3 = held.tile([P, 2 * C], F32, name="y3")
        y1 = [held.tile([P, C], F32, name=f"y1{i}") for i in range(3)]
        y2 = [held.tile([P, 2 * C], F32, name=f"y2{i}") for i in range(4)]

        def gather0(j):
            for lo, hi in ((0, 128), (128, 256)) if j == 3 else ((0, 256),):
                nc.vector.tensor_copy(grouped0[:, lo:hi, j], planes[j][:].indirect(columns(offs_t, lo, hi)))

        for j in range(3):
            gather0(j)
            nc.gpsimd.tensor_scalar(halves[j][:], planes[j][:], 1.0, 0.0, op0=MULT, op1=ADD)
        gather0(3)
        quantize(codes[0], scales[0], grouped0, 0, 128)
        quantize(codes[0], scales[0], grouped0, 128, 256)
        halves.append(held.tile([P, T], BF16, name="half3", tag="g0", align_bytes=64))
        nc.vector.tensor_copy(halves[3][:], planes[3][:])
        acc = psum.tile([P, 512], F32, name="acc")
        multiply(acc[:, 0:128], q[0], 0, 128, 0, 0)
        add_bias(ya[:], acc[:, 0:128], 0, 0)
        for i, y in ((1, y01[:]), (2, y02[:]), (3, y3[:, 0:C])):
            acc = psum.tile([P, 512], F32, name="acc")
            multiply(acc[:, 0:C], q[0], 0, C, 0, i)
            add_bias(y, acc[:, 0:C], 0, i)
            if i == 1:
                acc = psum.tile([P, 512], F32, name="acc")
                multiply(acc[:, 0:128], q[0], 128, C, 0, 0)
                add_bias(yb[:], acc[:, 0:128], 0, 0)
        for j in range(PACK):
            gather_scalar(grouped1, 256, 512, j)
        scatter(w0, ya[:], 0, 128)
        scatter(w1, y01[:], 0, 256)
        scatter(w0, yb[:], 128, 256)
        quantize(codes[1], scales[1], grouped1, 0, C)
        for i, y in enumerate((y1[0][:], y1[1][:], y1[2][:], y3[:, C : 2 * C])):
            acc = psum.tile([P, 512], F32, name="acc")
            multiply(acc[:, 0:C], q[1], 0, C, 1, i)
            add_bias(y, acc[:, 0:C], 1, i)
        w2 = held.tile([P, T], F32, name="w2", tag="w2", align_bytes=64)
        scatter(w2, y02[:], 0, 256)
        grouped2 = held.tile([P, 2 * C, PACK], BF16, name="grouped2", tag="w3", align_bytes=64)
        for j in range(PACK):
            gather_scalar(grouped2, 512, 1024, j)
        scatter(w0, y1[0][:], 256, 512)
        scatter(w1, y1[1][:], 256, 512)
        scatter(w2, y1[2][:], 256, 512)
        quantize(codes[2], scales[2], grouped2, 0, 2 * C)
        for i in range(N_TILES):
            acc = psum.tile([P, 512], F32, name="acc")
            for e in (2, 3):
                lo = (e - 2) * C
                multiply(acc[:, lo : lo + C], q[2], lo, lo + C, e, i)
            for e in (2, 3):
                lo = (e - 2) * C
                add_bias(y2[i][:, lo : lo + C], acc[:, lo : lo + C], e, i)
        w3 = held.tile([P, T], F32, name="w3", tag="w3", align_bytes=64)
        scatter(w3, y3[:], 0, 512)
        for i, window in enumerate((w0, w1, w2, w3)):
            scatter(window, y2[i][:], 512, 1024)
            nc.sync.dma_start(out=out[P * i : P * (i + 1), :], in_=window[:])
